import numpy as np
import ml_dtypes


def mxq(x, axis, fmt="e4m3"):
    dtype, down = {"e4m3": (ml_dtypes.float8_e4m3fn, 7), "e5m2": (ml_dtypes.float8_e5m2, 14)}[fmt]
    v = np.moveaxis(np.asarray(x, np.float32).astype(ml_dtypes.bfloat16).astype(np.float64), axis, -1)
    blocks = v.reshape(v.shape[:-1] + (-1, 32))
    amax = np.abs(blocks).max(-1, keepdims=True)
    byte = np.maximum(np.where(amax > 0, np.frexp(amax)[1] - 1 + 127, 0) - down, 1)
    scale = np.exp2(byte - 127.0)
    codes = (blocks / scale).astype(np.float32).astype(dtype).astype(np.float64)
    return np.moveaxis((codes * scale).reshape(v.shape), -1, axis)


WIDE = False


def mx_kscale(k, group=512):
    if not WIDE:
        return np.ones(k)
    levels = np.array([10, -10, 5, -5, 0])
    if group != 512:
        return np.exp2(np.random.permutation(np.resize(levels, k // group))).repeat(group)
    if k % 512:
        return np.exp2(np.random.permutation(np.resize(levels, k // 32))).repeat(32)
    a = np.empty((k // 512, 16))
    for p in range(k // 512):
        a[p, :8] = np.random.permutation(np.resize(levels, 8))
        for g in range(8):
            far = levels[np.abs(levels - a[p, g]) >= 10]
            a[p, g + 8] = far[np.random.randint(len(far))]
    return np.exp2(a.ravel()).repeat(32)


def f64(x):
    return np.asarray(x).astype(np.float64)


E2M1 = np.array([0.0, 0.5, 1.0, 1.5, 2.0, 3.0, 4.0, 6.0, -0.0, -0.5, -1.0, -1.5, -2.0, -3.0, -4.0, -6.0])


def pack_group(w):
    k, n = w.shape
    w = f64(np.asarray(w, np.float32).astype(ml_dtypes.bfloat16)).reshape(k // 32, 32, n)
    amax = np.abs(w).max(1)
    mant, ex = np.frexp(amax / 6.0)
    byte = np.clip(np.where(amax > 0, np.where(mant > 0.5, ex, ex - 1) + 127, 1), 1, 254)
    scaled = (w * np.exp2(127.0 - byte)[:, None, :]).reshape(k, n).astype(np.float32)
    c = np.ascontiguousarray(scaled.reshape(k // 4, 4, n).transpose(0, 2, 1)).astype(ml_dtypes.float4_e2m1fn).view(np.uint8) & 0xF
    return np.ascontiguousarray((c[..., 0::2] | (c[..., 1::2] << 4)).reshape(k // 4, 2 * n)), byte.astype(np.uint8)


def unpack_group(words, scales):
    p, n = words.shape[0], scales.shape[1]
    words = np.ascontiguousarray(words).reshape(p, n, 2)
    nib = np.empty((p, n, 4), np.uint8)
    nib[..., 0::2] = words & 0xF
    nib[..., 1::2] = words >> 4
    return E2M1[nib].transpose(0, 2, 1).reshape(4 * p, n) * np.repeat(np.exp2(scales.astype(np.float64) - 127.0), 32, axis=0)


G, D, M, N = 2, 256, 256, 512


def setup_inputs():
    n = np.random.standard_normal
    s = mx_kscale(D, 0)[:, None]
    w_ = [pack_group(w) for w in n((G, D, M)) / np.sqrt(D) / s]
    return {
        "x": (n((G, D, N)) * s).astype(np.float32),
        "w_words": np.stack([w[0] for w in w_]),
        "w_scales": np.stack([w[1] for w in w_]),
        "r": n((G, M, N)).astype(np.float32),
    }


def reference(x, w_words, w_scales, r):
    xq = mxq(f64(x), 1, "e4m3")
    y = np.stack([unpack_group(w_words[g], w_scales[g]) for g in range(G)]).transpose(0, 2, 1) @ xq
    y = y + f64(r)
    return y

@@ -1,0 +1,95 @@
+from contextlib import ExitStack
+
+import concourse.mybir as mybir
+
+G, D, M, N = 2, 256, 256, 512
+FLOPS = 2 * G * D * M * N
+
+F32 = mybir.dt.float32
+BF16 = mybir.dt.bfloat16
+I32 = mybir.dt.int32
+U32 = mybir.dt.uint32
+U8 = mybir.dt.uint8
+FP8X4 = mybir.dt.float8_e4m3fn_x4
+FP4X4 = mybir.dt.float4_e2m1fn_x4
+
+P = 128
+PACK = 4
+ROWS = D // PACK
+CHUNK = 256
+VEC_COLS = 160
+
+
+def tile_rows_glin_res_kernel(tc, x, w_words, w_scales, r, out):
+    nc = tc.nc
+    with ExitStack() as ctx:
+        sb = ctx.enter_context(tc.tile_pool(name="sb", bufs=1))
+        ps = ctx.enter_context(tc.psum_pool(name="ps", bufs=1))
+        ctx.enter_context(tc.manual_schedule())
+
+        w_sb = sb.tile([P, 2 * M], U8, name="w_sb", align_bytes=64)
+        w_sc = sb.tile([P, M], U8, name="w_sc", align_bytes=64)
+        codes = sb.tile([P, N], U32, name="codes", align_bytes=64)
+        x_sc = sb.tile([P, N], U8, name="x_sc", align_bytes=64)
+
+        nc.vector.memset(w_sc[:].bitcast(I32), 0)
+        sc_rows = w_scales.rearrange("g (h i) m -> i (g h) m", i=4)
+        for i in range(4):
+            nc.scalar.dma_start(out=w_sc[i:P:32, :].bitcast(I32), in_=sc_rows[i].bitcast(I32))
+
+        x_rows = x.rearrange("g (p j) n -> (g p) j n", j=PACK)
+        raws = []
+        for c in range(N // CHUNK):
+            raw = sb.tile([P, PACK, CHUNK], F32, name="raw%d" % c)
+            nc.sync.dma_start(out=raw[:], in_=x_rows[:, :, c * CHUNK:(c + 1) * CHUNK])
+            raws.append(raw)
+        nc.sync.dma_start(out=w_sb[:].bitcast(I32), in_=w_words.rearrange("g p b -> (g p) b").bitcast(I32))
+
+        blocks = [(g, h) for h in range(M // P) for g in range(G)]
+        res = []
+        for g, h in blocks:
+            rt = sb.tile([P, N], F32, name="r%d%d" % (g, h))
+            nc.sync.dma_start(out=rt[:], in_=r[g, h * P:(h + 1) * P, :])
+            res.append(rt)
+
+        for c in range(N // CHUNK):
+            grouped = sb.tile([P, CHUNK, PACK], BF16, name="grouped%d" % c, align_bytes=64)
+            raw = raws[c]
+            nc.scalar.copy(
+                out=grouped[:, VEC_COLS:, :].rearrange("p (c i) t -> p c t i", i=4),
+                in_=raw[:, :, VEC_COLS:].rearrange("p t (c i) -> p c t i", i=4),
+            )
+            nc.vector.tensor_copy(
+                out=grouped[:, :VEC_COLS, :].rearrange("p (c i) t -> p c t i", i=4),
+                in_=raw[:, :, :VEC_COLS].rearrange("p t (c i) -> p c t i", i=4),
+            )
+            cols = slice(c * CHUNK, (c + 1) * CHUNK)
+            nc.vector.quantize_mx(
+                out=codes[:, cols].bitcast(FP8X4),
+                scales=x_sc[:, cols],
+                in_=grouped[:].rearrange("p n t -> p (n t)"),
+            )
+
+        accs = []
+        for g, h in blocks:
+            acc = ps.tile([P, N], F32, name="acc%d%d" % (g, h))
+            rows = slice(g * ROWS, (g + 1) * ROWS)
+            nc.tensor.matmul_mx(
+                out=acc[:],
+                lhsT=w_sb[rows, 2 * h * P:2 * (h + 1) * P].bitcast(FP4X4),
+                lhsT_scale=w_sc[rows, h * P:(h + 1) * P],
+                rhs=codes[rows, :].bitcast(FP8X4),
+                rhs_scale=x_sc[rows, :],
+                start=True,
+                stop=True,
+            )
+            accs.append(acc)
+
+        for b, (g, h) in enumerate(blocks):
+            parts = 2 if b in (0, len(blocks) - 1) else 1
+            width = N // parts
+            for s in range(parts):
+                cols = slice(s * width, (s + 1) * width)
+                o = sb.tile([P, width], F32, name="o%d%d" % (b, s))
+                nc.vector.tensor_add(out=o[:], in0=accs[b][:, cols], in1=res[b][:, cols])
+                nc.sync.dma_start(out=out[g, h * P:(h + 1) * P, cols], in_=o[:])

@@ -16,8 +16,8 @@ FP4X4 = mybir.dt.float4_e2m1fn_x4
 P = 128
 PACK = 4
 ROWS = D // PACK
-CHUNK = 256
-VEC_COLS = 160
+HALF = N // 2
+VEC_COLS = (160, 144)
 
 
 def tile_rows_glin_res_kernel(tc, x, w_words, w_scales, r, out):
@@ -29,67 +29,87 @@ def tile_rows_glin_res_kernel(tc, x, w_words, w_scales, r, out):
 
         w_sb = sb.tile([P, 2 * M], U8, name="w_sb", align_bytes=64)
         w_sc = sb.tile([P, M], U8, name="w_sc", align_bytes=64)
-        codes = sb.tile([P, N], U32, name="codes", align_bytes=64)
-        x_sc = sb.tile([P, N], U8, name="x_sc", align_bytes=64)
+        codes = sb.tile([P, HALF + N], U32, name="codes", align_bytes=64)
+        x_sc = sb.tile([P, HALF + N], U8, name="x_sc", align_bytes=64)
 
         nc.vector.memset(w_sc[:].bitcast(I32), 0)
+        nc.vector.memset(codes[:, :HALF], 0)
+        nc.vector.memset(x_sc[:, :HALF].bitcast(I32), 0)
         sc_rows = w_scales.rearrange("g (h i) m -> i (g h) m", i=4)
         for i in range(4):
             nc.scalar.dma_start(out=w_sc[i:P:32, :].bitcast(I32), in_=sc_rows[i].bitcast(I32))
 
         x_rows = x.rearrange("g (p j) n -> (g p) j n", j=PACK)
         raws = []
-        for c in range(N // CHUNK):
-            raw = sb.tile([P, PACK, CHUNK], F32, name="raw%d" % c)
-            nc.sync.dma_start(out=raw[:], in_=x_rows[:, :, c * CHUNK:(c + 1) * CHUNK])
+        for c in range(2):
+            raw = sb.tile([P, PACK, HALF], F32, name="raw%d" % c)
+            nc.sync.dma_start(out=raw[:], in_=x_rows[:, :, c * HALF:(c + 1) * HALF])
             raws.append(raw)
-        nc.sync.dma_start(out=w_sb[:].bitcast(I32), in_=w_words.rearrange("g p b -> (g p) b").bitcast(I32))
+            if c == 0:
+                nc.sync.dma_start(out=w_sb[:].bitcast(I32), in_=w_words.rearrange("g p b -> (g p) b").bitcast(I32))
 
-        blocks = [(g, h) for h in range(M // P) for g in range(G)]
-        res = []
-        for g, h in blocks:
-            rt = sb.tile([P, N], F32, name="r%d%d" % (g, h))
-            nc.sync.dma_start(out=rt[:], in_=r[g, h * P:(h + 1) * P, :])
-            res.append(rt)
+        res = {}
+        for c in range(2):
+            for h in range(2):
+                rt = sb.tile([P, G, HALF], F32, name="r%d%d" % (c, h))
+                nc.sync.dma_start(
+                    out=rt[:],
+                    in_=r[:, h * P:(h + 1) * P, c * HALF:(c + 1) * HALF].rearrange("g p n -> p g n"),
+                )
+                res[(c, h)] = rt
 
-        for c in range(N // CHUNK):
-            grouped = sb.tile([P, CHUNK, PACK], BF16, name="grouped%d" % c, align_bytes=64)
-            raw = raws[c]
+        grouped = {}
+        accs = {}
+
+        def interleave(c):
+            gt = sb.tile([P, HALF, PACK], BF16, name="grouped%d" % c, align_bytes=64)
+            v = VEC_COLS[c]
             nc.scalar.copy(
-                out=grouped[:, VEC_COLS:, :].rearrange("p (c i) t -> p c t i", i=4),
-                in_=raw[:, :, VEC_COLS:].rearrange("p t (c i) -> p c t i", i=4),
+                out=gt[:, v:, :].rearrange("p (c i) t -> p c t i", i=4),
+                in_=raws[c][:, :, v:].rearrange("p t (c i) -> p c t i", i=4),
             )
             nc.vector.tensor_copy(
-                out=grouped[:, :VEC_COLS, :].rearrange("p (c i) t -> p c t i", i=4),
-                in_=raw[:, :, :VEC_COLS].rearrange("p t (c i) -> p c t i", i=4),
+                out=gt[:, :v, :].rearrange("p (c i) t -> p c t i", i=4),
+                in_=raws[c][:, :, :v].rearrange("p t (c i) -> p c t i", i=4),
             )
-            cols = slice(c * CHUNK, (c + 1) * CHUNK)
+            grouped[c] = gt
+
+        def multiply(c):
+            cols = slice((c + 1) * HALF, (c + 2) * HALF)
             nc.vector.quantize_mx(
                 out=codes[:, cols].bitcast(FP8X4),
                 scales=x_sc[:, cols],
-                in_=grouped[:].rearrange("p n t -> p (n t)"),
+                in_=grouped[c][:].rearrange("p n t -> p (n t)"),
             )
+            window = slice(c * HALF, c * HALF + N)
+            for h in range(2):
+                for g in range(G):
+                    acc = ps.tile([P, N], F32, name="acc%d%d%d" % (c, h, g))
+                    rows = slice(g * ROWS, (g + 1) * ROWS)
+                    nc.tensor.matmul_mx(
+                        out=acc[:],
+                        lhsT=w_sb[rows, 2 * h * P:2 * (h + 1) * P].bitcast(FP4X4),
+                        lhsT_scale=w_sc[rows, h * P:(h + 1) * P],
+                        rhs=codes[rows, window].bitcast(FP8X4),
+                        rhs_scale=x_sc[rows, window],
+                        start=True,
+                        stop=True,
+                    )
+                    accs[(c, h, g)] = acc
 
-        accs = []
-        for g, h in blocks:
-            acc = ps.tile([P, N], F32, name="acc%d%d" % (g, h))
-            rows = slice(g * ROWS, (g + 1) * ROWS)
-            nc.tensor.matmul_mx(
-                out=acc[:],
-                lhsT=w_sb[rows, 2 * h * P:2 * (h + 1) * P].bitcast(FP4X4),
-                lhsT_scale=w_sc[rows, h * P:(h + 1) * P],
-                rhs=codes[rows, :].bitcast(FP8X4),
-                rhs_scale=x_sc[rows, :],
-                start=True,
-                stop=True,
-            )
-            accs.append(acc)
+        def finish(c, h, g):
+            o = sb.tile([P, HALF], F32, name="o%d%d%d" % (c, h, g))
+            nc.vector.tensor_add(out=o[:], in0=accs[(c, h, g)][:, HALF:], in1=res[(c, h)][:, g, :])
+            nc.sync.dma_start(out=out[g, h * P:(h + 1) * P, c * HALF:(c + 1) * HALF], in_=o[:])
 
-        for b, (g, h) in enumerate(blocks):
-            parts = 2 if b in (0, len(blocks) - 1) else 1
-            width = N // parts
-            for s in range(parts):
-                cols = slice(s * width, (s + 1) * width)
-                o = sb.tile([P, width], F32, name="o%d%d" % (b, s))
-                nc.vector.tensor_add(out=o[:], in0=accs[b][:, cols], in1=res[b][:, cols])
-                nc.sync.dma_start(out=out[g, h * P:(h + 1) * P, cols], in_=o[:])
+        interleave(0)
+        multiply(0)
+        interleave(1)
+        finish(0, 0, 0)
+        multiply(1)
+        finish(0, 0, 1)
+        finish(0, 1, 0)
+        finish(0, 1, 1)
+        for h in range(2):
+            for g in range(G):
+                finish(1, h, g)

@@ -36,8 +36,6 @@ def tile_rows_glin_res_kernel(tc, x, w_words, w_scales, r, out):
         nc.vector.memset(codes[:, :HALF], 0)
         nc.vector.memset(x_sc[:, :HALF].bitcast(I32), 0)
         sc_rows = w_scales.rearrange("g (h i) m -> i (g h) m", i=4)
-        for i in range(4):
-            nc.scalar.dma_start(out=w_sc[i:P:32, :].bitcast(I32), in_=sc_rows[i].bitcast(I32))
 
         x_rows = x.rearrange("g (p j) n -> (g p) j n", j=PACK)
         raws = []
@@ -46,6 +44,8 @@ def tile_rows_glin_res_kernel(tc, x, w_words, w_scales, r, out):
             nc.sync.dma_start(out=raw[:], in_=x_rows[:, :, c * HALF:(c + 1) * HALF])
             raws.append(raw)
             if c == 0:
+                for i in range(4):
+                    nc.sync.dma_start(out=w_sc[i:P:32, :].bitcast(I32), in_=sc_rows[i].bitcast(I32))
                 nc.sync.dma_start(out=w_sb[:].bitcast(I32), in_=w_words.rearrange("g p b -> (g p) b").bitcast(I32))
 
         res = {}

@@ -17,7 +17,7 @@ P = 128
 PACK = 4
 ROWS = D // PACK
 HALF = N // 2
-VEC_COLS = (160, 144)
+VEC_COLS = (160, 136)
 
 
 def tile_rows_glin_res_kernel(tc, x, w_words, w_scales, r, out):
@@ -46,7 +46,7 @@ def tile_rows_glin_res_kernel(tc, x, w_words, w_scales, r, out):
             if c == 0:
                 for i in range(4):
                     nc.sync.dma_start(out=w_sc[i:P:32, :].bitcast(I32), in_=sc_rows[i].bitcast(I32))
-                nc.sync.dma_start(out=w_sb[:].bitcast(I32), in_=w_words.rearrange("g p b -> (g p) b").bitcast(I32))
+        nc.sync.dma_start(out=w_sb[:].bitcast(I32), in_=w_words.rearrange("g p b -> (g p) b").bitcast(I32))
 
         res = {}
         for c in range(2):
@@ -105,8 +105,8 @@ def tile_rows_glin_res_kernel(tc, x, w_words, w_scales, r, out):
         interleave(0)
         multiply(0)
         interleave(1)
-        finish(0, 0, 0)
         multiply(1)
+        finish(0, 0, 0)
         finish(0, 0, 1)
         finish(0, 1, 0)
         finish(0, 1, 1)

@@ -36,17 +36,27 @@ def tile_rows_glin_res_kernel(tc, x, w_words, w_scales, r, out):
         nc.vector.memset(codes[:, :HALF], 0)
         nc.vector.memset(x_sc[:, :HALF].bitcast(I32), 0)
         sc_rows = w_scales.rearrange("g (h i) m -> i (g h) m", i=4)
-
         x_rows = x.rearrange("g (p j) n -> (g p) j n", j=PACK)
-        raws = []
-        for c in range(2):
-            raw = sb.tile([P, PACK, HALF], F32, name="raw%d" % c)
-            nc.sync.dma_start(out=raw[:], in_=x_rows[:, :, c * HALF:(c + 1) * HALF])
-            raws.append(raw)
-            if c == 0:
-                for i in range(4):
-                    nc.sync.dma_start(out=w_sc[i:P:32, :].bitcast(I32), in_=sc_rows[i].bitcast(I32))
-        nc.sync.dma_start(out=w_sb[:].bitcast(I32), in_=w_words.rearrange("g p b -> (g p) b").bitcast(I32))
+        pieces = ((0, HALF), (HALF, N))
+        raws = {}
+
+        def load_x(k):
+            lo, hi = pieces[k]
+            raw = sb.tile([P, PACK, hi - lo], F32, name="raw%d" % k)
+            nc.sync.dma_start(out=raw[:], in_=x_rows[:, :, lo:hi])
+            raws[k] = raw
+
+        def load_scales():
+            for i in range(4):
+                nc.sync.dma_start(out=w_sc[i:P:32, :].bitcast(I32), in_=sc_rows[i].bitcast(I32))
+
+        def load_words():
+            nc.sync.dma_start(out=w_sb[:].bitcast(I32), in_=w_words.rearrange("g p b -> (g p) b").bitcast(I32))
+
+        load_x(0)
+        load_scales()
+        load_x(1)
+        load_words()
 
         res = {}
         for c in range(2):
@@ -58,58 +68,60 @@ def tile_rows_glin_res_kernel(tc, x, w_words, w_scales, r, out):
                 )
                 res[(c, h)] = rt
 
-        grouped = {}
         accs = {}
+        grouped = {}
 
-        def interleave(c):
-            gt = sb.tile([P, HALF, PACK], BF16, name="grouped%d" % c, align_bytes=64)
-            v = VEC_COLS[c]
-            nc.scalar.copy(
-                out=gt[:, v:, :].rearrange("p (c i) t -> p c t i", i=4),
-                in_=raws[c][:, :, v:].rearrange("p t (c i) -> p c t i", i=4),
+        def deal(copy, dst, src):
+            copy(
+                out=dst.rearrange("p (c i) t -> p c t i", i=4),
+                in_=src.rearrange("p t (c i) -> p c t i", i=4),
             )
-            nc.vector.tensor_copy(
-                out=gt[:, :v, :].rearrange("p (c i) t -> p c t i", i=4),
-                in_=raws[c][:, :, :v].rearrange("p t (c i) -> p c t i", i=4),
-            )
-            grouped[c] = gt
 
-        def multiply(c):
-            cols = slice((c + 1) * HALF, (c + 2) * HALF)
+        def interleave(k):
+            lo, hi = pieces[k]
+            gt = sb.tile([P, hi - lo, PACK], BF16, name="grouped%d" % k, align_bytes=64)
+            v = VEC_COLS[k]
+            if v < hi - lo:
+                deal(nc.scalar.copy, gt[:, v:, :], raws[k][:, :, v:])
+            deal(nc.vector.tensor_copy, gt[:, :v, :], raws[k][:, :, :v])
+            grouped[k] = gt
+
+        def quantise(k):
+            lo, hi = pieces[k]
+            cols = slice(HALF + lo, HALF + hi)
             nc.vector.quantize_mx(
                 out=codes[:, cols].bitcast(FP8X4),
                 scales=x_sc[:, cols],
-                in_=grouped[c][:].rearrange("p n t -> p (n t)"),
+                in_=grouped[k][:].rearrange("p n t -> p (n t)"),
             )
+
+        def multiply(c, h):
             window = slice(c * HALF, c * HALF + N)
-            for h in range(2):
-                for g in range(G):
-                    acc = ps.tile([P, N], F32, name="acc%d%d%d" % (c, h, g))
-                    rows = slice(g * ROWS, (g + 1) * ROWS)
-                    nc.tensor.matmul_mx(
-                        out=acc[:],
-                        lhsT=w_sb[rows, 2 * h * P:2 * (h + 1) * P].bitcast(FP4X4),
-                        lhsT_scale=w_sc[rows, h * P:(h + 1) * P],
-                        rhs=codes[rows, window].bitcast(FP8X4),
-                        rhs_scale=x_sc[rows, window],
-                        start=True,
-                        stop=True,
-                    )
-                    accs[(c, h, g)] = acc
+            for g in range(G):
+                acc = ps.tile([P, N], F32, name="acc%d%d%d" % (c, h, g))
+                rows = slice(g * ROWS, (g + 1) * ROWS)
+                nc.tensor.matmul_mx(
+                    out=acc[:],
+                    lhsT=w_sb[rows, 2 * h * P:2 * (h + 1) * P].bitcast(FP4X4),
+                    lhsT_scale=w_sc[rows, h * P:(h + 1) * P],
+                    rhs=codes[rows, window].bitcast(FP8X4),
+                    rhs_scale=x_sc[rows, window],
+                    start=True,
+                    stop=True,
+                )
+                accs[(c, h, g)] = acc
 
         def finish(c, h, g):
             o = sb.tile([P, HALF], F32, name="o%d%d%d" % (c, h, g))
             nc.vector.tensor_add(out=o[:], in0=accs[(c, h, g)][:, HALF:], in1=res[(c, h)][:, g, :])
             nc.sync.dma_start(out=out[g, h * P:(h + 1) * P, c * HALF:(c + 1) * HALF], in_=o[:])
 
-        interleave(0)
-        multiply(0)
-        interleave(1)
-        multiply(1)
-        finish(0, 0, 0)
-        finish(0, 0, 1)
-        finish(0, 1, 0)
-        finish(0, 1, 1)
-        for h in range(2):
-            for g in range(G):
-                finish(1, h, g)
+        for c in range(2):
+            interleave(c)
+            quantise(c)
+            for h in range(2):
+                multiply(c, h)
+        for c in range(2):
+            for h in range(2):
+                for g in reversed(range(G)):
+                    finish(c, h, g)

@@ -17,7 +17,8 @@ P = 128
 PACK = 4
 ROWS = D // PACK
 HALF = N // 2
-VEC_COLS = (160, 136)
+QUARTER = N // 4
+VEC_COLS = (160, 80, 56)
 
 
 def tile_rows_glin_res_kernel(tc, x, w_words, w_scales, r, out):
@@ -37,7 +38,7 @@ def tile_rows_glin_res_kernel(tc, x, w_words, w_scales, r, out):
         nc.vector.memset(x_sc[:, :HALF].bitcast(I32), 0)
         sc_rows = w_scales.rearrange("g (h i) m -> i (g h) m", i=4)
         x_rows = x.rearrange("g (p j) n -> (g p) j n", j=PACK)
-        pieces = ((0, HALF), (HALF, N))
+        pieces = ((0, HALF), (HALF, HALF + QUARTER), (HALF + QUARTER, N))
         raws = {}
 
         def load_x(k):
@@ -55,8 +56,9 @@ def tile_rows_glin_res_kernel(tc, x, w_words, w_scales, r, out):
 
         load_x(0)
         load_scales()
-        load_x(1)
         load_words()
+        load_x(1)
+        load_x(2)
 
         res = {}
         for c in range(2):
@@ -116,11 +118,16 @@ def tile_rows_glin_res_kernel(tc, x, w_words, w_scales, r, out):
             nc.vector.tensor_add(out=o[:], in0=accs[(c, h, g)][:, HALF:], in1=res[(c, h)][:, g, :])
             nc.sync.dma_start(out=out[g, h * P:(h + 1) * P, c * HALF:(c + 1) * HALF], in_=o[:])
 
-        for c in range(2):
-            interleave(c)
-            quantise(c)
-            for h in range(2):
-                multiply(c, h)
+        interleave(0)
+        quantise(0)
+        multiply(0, 0)
+        multiply(0, 1)
+        interleave(1)
+        interleave(2)
+        quantise(1)
+        quantise(2)
+        multiply(1, 0)
+        multiply(1, 1)
         for c in range(2):
             for h in range(2):
                 for g in reversed(range(G)):

@@ -18,7 +18,7 @@ PACK = 4
 ROWS = D // PACK
 HALF = N // 2
 QUARTER = N // 4
-VEC_COLS = (160, 80, 56)
+VEC_COLS = (80, 56, 80, 56)
 
 
 def tile_rows_glin_res_kernel(tc, x, w_words, w_scales, r, out):
@@ -38,7 +38,7 @@ def tile_rows_glin_res_kernel(tc, x, w_words, w_scales, r, out):
         nc.vector.memset(x_sc[:, :HALF].bitcast(I32), 0)
         sc_rows = w_scales.rearrange("g (h i) m -> i (g h) m", i=4)
         x_rows = x.rearrange("g (p j) n -> (g p) j n", j=PACK)
-        pieces = ((0, HALF), (HALF, HALF + QUARTER), (HALF + QUARTER, N))
+        pieces = [(k * QUARTER, (k + 1) * QUARTER) for k in range(4)]
         raws = {}
 
         def load_x(k):
@@ -54,11 +54,12 @@ def tile_rows_glin_res_kernel(tc, x, w_words, w_scales, r, out):
         def load_words():
             nc.sync.dma_start(out=w_sb[:].bitcast(I32), in_=w_words.rearrange("g p b -> (g p) b").bitcast(I32))
 
-        load_x(0)
-        load_scales()
         load_words()
+        load_x(0)
         load_x(1)
+        load_scales()
         load_x(2)
+        load_x(3)
 
         res = {}
         for c in range(2):
@@ -118,17 +119,14 @@ def tile_rows_glin_res_kernel(tc, x, w_words, w_scales, r, out):
             nc.vector.tensor_add(out=o[:], in0=accs[(c, h, g)][:, HALF:], in1=res[(c, h)][:, g, :])
             nc.sync.dma_start(out=out[g, h * P:(h + 1) * P, c * HALF:(c + 1) * HALF], in_=o[:])
 
-        interleave(0)
-        quantise(0)
-        multiply(0, 0)
-        multiply(0, 1)
-        interleave(1)
-        interleave(2)
-        quantise(1)
-        quantise(2)
-        multiply(1, 0)
-        multiply(1, 1)
+        for c in range(2):
+            interleave(2 * c)
+            interleave(2 * c + 1)
+            quantise(2 * c)
+            quantise(2 * c + 1)
+            for h in range(2):
+                multiply(c, h)
         for c in range(2):
             for h in range(2):
-                for g in reversed(range(G)):
+                for g in range(G):
                     finish(c, h, g)

@@ -62,14 +62,15 @@ def tile_rows_glin_res_kernel(tc, x, w_words, w_scales, r, out):
         load_x(3)
 
         res = {}
-        for c in range(2):
-            for h in range(2):
-                rt = sb.tile([P, G, HALF], F32, name="r%d%d" % (c, h))
-                nc.sync.dma_start(
-                    out=rt[:],
-                    in_=r[:, h * P:(h + 1) * P, c * HALF:(c + 1) * HALF].rearrange("g p n -> p g n"),
-                )
-                res[(c, h)] = rt
+        first = sb.tile([P, G, HALF], F32, name="r00")
+        nc.sync.dma_start(out=first[:], in_=r[:, :P, :HALF].rearrange("g p n -> p g n"))
+        for g in range(G):
+            res[(0, 0, g)] = first[:, g, :]
+        for c, h in ((0, 1), (1, 0), (1, 1)):
+            for g in range(G):
+                rt = sb.tile([P, HALF], F32, name="r%d%d%d" % (c, h, g))
+                nc.sync.dma_start(out=rt[:], in_=r[g, h * P:(h + 1) * P, c * HALF:(c + 1) * HALF])
+                res[(c, h, g)] = rt[:]
 
         accs = {}
         grouped = {}
@@ -100,7 +101,7 @@ def tile_rows_glin_res_kernel(tc, x, w_words, w_scales, r, out):
 
         def multiply(c, h):
             window = slice(c * HALF, c * HALF + N)
-            for g in range(G):
+            for g in reversed(range(G)):
                 acc = ps.tile([P, N], F32, name="acc%d%d%d" % (c, h, g))
                 rows = slice(g * ROWS, (g + 1) * ROWS)
                 nc.tensor.matmul_mx(
@@ -116,7 +117,7 @@ def tile_rows_glin_res_kernel(tc, x, w_words, w_scales, r, out):
 
         def finish(c, h, g):
             o = sb.tile([P, HALF], F32, name="o%d%d%d" % (c, h, g))
-            nc.vector.tensor_add(out=o[:], in0=accs[(c, h, g)][:, HALF:], in1=res[(c, h)][:, g, :])
+            nc.vector.tensor_add(out=o[:], in0=accs[(c, h, g)][:, HALF:], in1=res[(c, h, g)])
             nc.sync.dma_start(out=out[g, h * P:(h + 1) * P, c * HALF:(c + 1) * HALF], in_=o[:])
 
         for c in range(2):

@@ -17,8 +17,10 @@ P = 128
 PACK = 4
 ROWS = D // PACK
 HALF = N // 2
-QUARTER = N // 4
-VEC_COLS = (80, 56, 80, 56)
+PIECE = N // 4
+SCALE_ROWS = 4
+RUN = 4
+VEC_COLS = 72
 
 
 def tile_rows_glin_res_kernel(tc, x, w_words, w_scales, r, out):
@@ -36,28 +38,21 @@ def tile_rows_glin_res_kernel(tc, x, w_words, w_scales, r, out):
         nc.vector.memset(w_sc[:].bitcast(I32), 0)
         nc.vector.memset(codes[:, :HALF], 0)
         nc.vector.memset(x_sc[:, :HALF].bitcast(I32), 0)
-        sc_rows = w_scales.rearrange("g (h i) m -> i (g h) m", i=4)
+
         x_rows = x.rearrange("g (p j) n -> (g p) j n", j=PACK)
-        pieces = [(k * QUARTER, (k + 1) * QUARTER) for k in range(4)]
         raws = {}
 
         def load_x(k):
-            lo, hi = pieces[k]
-            raw = sb.tile([P, PACK, hi - lo], F32, name="raw%d" % k)
-            nc.sync.dma_start(out=raw[:], in_=x_rows[:, :, lo:hi])
+            raw = sb.tile([P, PACK, PIECE], F32, name="raw%d" % k)
+            nc.sync.dma_start(out=raw[:], in_=x_rows[:, :, k * PIECE:(k + 1) * PIECE])
             raws[k] = raw
 
-        def load_scales():
-            for i in range(4):
-                nc.sync.dma_start(out=w_sc[i:P:32, :].bitcast(I32), in_=sc_rows[i].bitcast(I32))
-
-        def load_words():
-            nc.sync.dma_start(out=w_sb[:].bitcast(I32), in_=w_words.rearrange("g p b -> (g p) b").bitcast(I32))
-
-        load_words()
+        nc.sync.dma_start(out=w_sb[:].bitcast(I32), in_=w_words.rearrange("g p b -> (g p) b").bitcast(I32))
         load_x(0)
         load_x(1)
-        load_scales()
+        sc_rows = w_scales.rearrange("g (q i) m -> i (g q) m", i=SCALE_ROWS)
+        for i in range(SCALE_ROWS):
+            nc.sync.dma_start(out=w_sc[i:P:32, :].bitcast(I32), in_=sc_rows[i].bitcast(I32))
         load_x(2)
         load_x(3)
 
@@ -75,24 +70,21 @@ def tile_rows_glin_res_kernel(tc, x, w_words, w_scales, r, out):
         accs = {}
         grouped = {}
 
-        def deal(copy, dst, src):
+        def round_and_group(copy, dst, src):
             copy(
-                out=dst.rearrange("p (c i) t -> p c t i", i=4),
-                in_=src.rearrange("p t (c i) -> p c t i", i=4),
+                out=dst.rearrange("p (c i) t -> p c t i", i=RUN),
+                in_=src.rearrange("p t (c i) -> p c t i", i=RUN),
             )
 
         def interleave(k):
-            lo, hi = pieces[k]
-            gt = sb.tile([P, hi - lo, PACK], BF16, name="grouped%d" % k, align_bytes=64)
-            v = VEC_COLS[k]
-            if v < hi - lo:
-                deal(nc.scalar.copy, gt[:, v:, :], raws[k][:, :, v:])
-            deal(nc.vector.tensor_copy, gt[:, :v, :], raws[k][:, :, :v])
+            gt = sb.tile([P, PIECE, PACK], BF16, name="grouped%d" % k, align_bytes=64)
+            v = VEC_COLS
+            round_and_group(nc.scalar.copy, gt[:, v:, :], raws[k][:, :, v:])
+            round_and_group(nc.vector.tensor_copy, gt[:, :v, :], raws[k][:, :, :v])
             grouped[k] = gt
 
         def quantise(k):
-            lo, hi = pieces[k]
-            cols = slice(HALF + lo, HALF + hi)
+            cols = slice(HALF + k * PIECE, HALF + (k + 1) * PIECE)
             nc.vector.quantize_mx(
                 out=codes[:, cols].bitcast(FP8X4),
                 scales=x_sc[:, cols],

@@ -49,23 +49,20 @@ def tile_rows_glin_res_kernel(tc, x, w_words, w_scales, r, out):
 
         nc.sync.dma_start(out=w_sb[:].bitcast(I32), in_=w_words.rearrange("g p b -> (g p) b").bitcast(I32))
         load_x(0)
-        load_x(1)
         sc_rows = w_scales.rearrange("g (q i) m -> i (g q) m", i=SCALE_ROWS)
         for i in range(SCALE_ROWS):
+            if i == SCALE_ROWS // 2:
+                load_x(1)
             nc.sync.dma_start(out=w_sc[i:P:32, :].bitcast(I32), in_=sc_rows[i].bitcast(I32))
         load_x(2)
         load_x(3)
 
+        order = [(0, 0, 0), (0, 0, 1), (0, 1, 0), (0, 1, 1), (1, 1, 1), (1, 1, 0), (1, 0, 0), (1, 0, 1)]
         res = {}
-        first = sb.tile([P, G, HALF], F32, name="r00")
-        nc.sync.dma_start(out=first[:], in_=r[:, :P, :HALF].rearrange("g p n -> p g n"))
-        for g in range(G):
-            res[(0, 0, g)] = first[:, g, :]
-        for c, h in ((0, 1), (1, 0), (1, 1)):
-            for g in range(G):
-                rt = sb.tile([P, HALF], F32, name="r%d%d%d" % (c, h, g))
-                nc.sync.dma_start(out=rt[:], in_=r[g, h * P:(h + 1) * P, c * HALF:(c + 1) * HALF])
-                res[(c, h, g)] = rt[:]
+        for c, h, g in order:
+            rt = sb.tile([P, HALF], F32, name="r%d%d%d" % (c, h, g))
+            nc.sync.dma_start(out=rt[:], in_=r[g, h * P:(h + 1) * P, c * HALF:(c + 1) * HALF])
+            res[(c, h, g)] = rt[:]
 
         accs = {}
         grouped = {}
@@ -93,7 +90,7 @@ def tile_rows_glin_res_kernel(tc, x, w_words, w_scales, r, out):
 
         def multiply(c, h):
             window = slice(c * HALF, c * HALF + N)
-            for g in reversed(range(G)):
+            for g in reversed([b[2] for b in order if b[:2] == (c, h)]):
                 acc = ps.tile([P, N], F32, name="acc%d%d%d" % (c, h, g))
                 rows = slice(g * ROWS, (g + 1) * ROWS)
                 nc.tensor.matmul_mx(
@@ -107,7 +104,15 @@ def tile_rows_glin_res_kernel(tc, x, w_words, w_scales, r, out):
                 )
                 accs[(c, h, g)] = acc
 
+        whole = sb.tile([P, N], F32, name="whole")
+
         def finish(c, h, g):
+            if (h, g) == (1, 1):
+                cols = slice(c * HALF, (c + 1) * HALF)
+                nc.vector.tensor_add(out=whole[:, cols], in0=accs[(c, h, g)][:, HALF:], in1=res[(c, h, g)])
+                if c == 1:
+                    nc.sync.dma_start(out=out[g, P:, :], in_=whole[:])
+                return
             o = sb.tile([P, HALF], F32, name="o%d%d%d" % (c, h, g))
             nc.vector.tensor_add(out=o[:], in0=accs[(c, h, g)][:, HALF:], in1=res[(c, h, g)])
             nc.sync.dma_start(out=out[g, h * P:(h + 1) * P, c * HALF:(c + 1) * HALF], in_=o[:])
@@ -117,9 +122,7 @@ def tile_rows_glin_res_kernel(tc, x, w_words, w_scales, r, out):
             interleave(2 * c + 1)
             quantise(2 * c)
             quantise(2 * c + 1)
-            for h in range(2):
+            for h in (c, 1 - c):
                 multiply(c, h)
-        for c in range(2):
-            for h in range(2):
-                for g in range(G):
-                    finish(c, h, g)
+        for c, h, g in order:
+            finish(c, h, g)

@@ -49,15 +49,16 @@ def tile_rows_glin_res_kernel(tc, x, w_words, w_scales, r, out):
 
         nc.sync.dma_start(out=w_sb[:].bitcast(I32), in_=w_words.rearrange("g p b -> (g p) b").bitcast(I32))
         load_x(0)
+        load_x(1)
         sc_rows = w_scales.rearrange("g (q i) m -> i (g q) m", i=SCALE_ROWS)
         for i in range(SCALE_ROWS):
-            if i == SCALE_ROWS // 2:
-                load_x(1)
             nc.sync.dma_start(out=w_sc[i:P:32, :].bitcast(I32), in_=sc_rows[i].bitcast(I32))
         load_x(2)
         load_x(3)
 
         order = [(0, 0, 0), (0, 0, 1), (0, 1, 0), (0, 1, 1), (1, 1, 1), (1, 1, 0), (1, 0, 0), (1, 0, 1)]
+        whole_rows = (1, 1)
+
         res = {}
         for c, h, g in order:
             rt = sb.tile([P, HALF], F32, name="r%d%d%d" % (c, h, g))
@@ -90,7 +91,7 @@ def tile_rows_glin_res_kernel(tc, x, w_words, w_scales, r, out):
 
         def multiply(c, h):
             window = slice(c * HALF, c * HALF + N)
-            for g in reversed([b[2] for b in order if b[:2] == (c, h)]):
+            for g in reversed([bank[2] for bank in order if bank[:2] == (c, h)]):
                 acc = ps.tile([P, N], F32, name="acc%d%d%d" % (c, h, g))
                 rows = slice(g * ROWS, (g + 1) * ROWS)
                 nc.tensor.matmul_mx(
@@ -107,15 +108,17 @@ def tile_rows_glin_res_kernel(tc, x, w_words, w_scales, r, out):
         whole = sb.tile([P, N], F32, name="whole")
 
         def finish(c, h, g):
-            if (h, g) == (1, 1):
-                cols = slice(c * HALF, (c + 1) * HALF)
-                nc.vector.tensor_add(out=whole[:, cols], in0=accs[(c, h, g)][:, HALF:], in1=res[(c, h, g)])
+            outputs = slice(h * P, (h + 1) * P)
+            cols = slice(c * HALF, (c + 1) * HALF)
+            sums = accs[(c, h, g)][:, HALF:]
+            if (h, g) == whole_rows:
+                nc.vector.tensor_add(out=whole[:, cols], in0=sums, in1=res[(c, h, g)])
                 if c == 1:
-                    nc.sync.dma_start(out=out[g, P:, :], in_=whole[:])
-                return
-            o = sb.tile([P, HALF], F32, name="o%d%d%d" % (c, h, g))
-            nc.vector.tensor_add(out=o[:], in0=accs[(c, h, g)][:, HALF:], in1=res[(c, h, g)])
-            nc.sync.dma_start(out=out[g, h * P:(h + 1) * P, c * HALF:(c + 1) * HALF], in_=o[:])
+                    nc.sync.dma_start(out=out[g, outputs, :], in_=whole[:])
+            else:
+                o = sb.tile([P, HALF], F32, name="o%d%d%d" % (c, h, g))
+                nc.vector.tensor_add(out=o[:], in0=sums, in1=res[(c, h, g)])
+                nc.sync.dma_start(out=out[g, outputs, cols], in_=o[:])
 
         for c in range(2):
             interleave(2 * c)

@@ -106,6 +106,8 @@ def tile_rows_glin_res_kernel(tc, x, w_words, w_scales, r, out):
                 accs[(c, h, g)] = acc
 
         whole = sb.tile([P, N], F32, name="whole")
+        last_pair = order[-1][:2]
+        pair = sb.tile([P, G, HALF], F32, name="pair")
 
         def finish(c, h, g):
             outputs = slice(h * P, (h + 1) * P)
@@ -115,6 +117,10 @@ def tile_rows_glin_res_kernel(tc, x, w_words, w_scales, r, out):
                 nc.vector.tensor_add(out=whole[:, cols], in0=sums, in1=res[(c, h, g)])
                 if c == 1:
                     nc.sync.dma_start(out=out[g, outputs, :], in_=whole[:])
+            elif (c, h) == last_pair:
+                nc.vector.tensor_add(out=pair[:, g, :], in0=sums, in1=res[(c, h, g)])
+                if (c, h, g) == order[-1]:
+                    nc.sync.dma_start(out=out.rearrange("g m n -> m g n")[outputs, :, cols], in_=pair[:])
             else:
                 o = sb.tile([P, HALF], F32, name="o%d%d%d" % (c, h, g))
                 nc.vector.tensor_add(out=o[:], in0=sums, in1=res[(c, h, g)])

@@ -17,10 +17,9 @@ P = 128
 PACK = 4
 ROWS = D // PACK
 HALF = N // 2
-PIECE = N // 4
 SCALE_ROWS = 4
 RUN = 4
-VEC_COLS = 72
+PIECES = ((128,72,),(128,72,),(128,72,),(64,40,),(64,40,),)
 
 
 def tile_rows_glin_res_kernel(tc, x, w_words, w_scales, r, out):
@@ -40,33 +39,61 @@ def tile_rows_glin_res_kernel(tc, x, w_words, w_scales, r, out):
         nc.vector.memset(x_sc[:, :HALF].bitcast(I32), 0)
 
         x_rows = x.rearrange("g (p j) n -> (g p) j n", j=PACK)
-        raws = {}
-
-        def load_x(k):
-            raw = sb.tile([P, PACK, PIECE], F32, name="raw%d" % k)
-            nc.sync.dma_start(out=raw[:], in_=x_rows[:, :, k * PIECE:(k + 1) * PIECE])
-            raws[k] = raw
-
-        nc.sync.dma_start(out=w_sb[:].bitcast(I32), in_=w_words.rearrange("g p b -> (g p) b").bitcast(I32))
-        load_x(0)
-        load_x(1)
         sc_rows = w_scales.rearrange("g (q i) m -> i (g q) m", i=SCALE_ROWS)
-        for i in range(SCALE_ROWS):
-            nc.sync.dma_start(out=w_sc[i:P:32, :].bitcast(I32), in_=sc_rows[i].bitcast(I32))
-        load_x(2)
-        load_x(3)
-
-        order = [(0, 0, 0), (0, 0, 1), (0, 1, 0), (0, 1, 1), (1, 1, 1), (1, 1, 0), (1, 0, 0), (1, 0, 1)]
-        whole_rows = (1, 1)
-
+        r_rows = r.rearrange("g (h p) n -> p (g h) n", p=P)
+        out_rows = out.rearrange("g (h p) n -> p (g h) n", p=P)
+        first = [sum(w for w, v in PIECES[:k]) for k in range(len(PIECES))]
+        raws = {}
         res = {}
-        for c, h, g in order:
-            rt = sb.tile([P, HALF], F32, name="r%d%d%d" % (c, h, g))
-            nc.sync.dma_start(out=rt[:], in_=r[g, h * P:(h + 1) * P, c * HALF:(c + 1) * HALF])
-            res[(c, h, g)] = rt[:]
-
         accs = {}
         grouped = {}
+        outs = {}
+
+        def load_x(k):
+            width = PIECES[k][0]
+            raw = sb.tile([P, PACK, width], F32, name="raw%d" % k)
+            nc.sync.dma_start(out=raw[:], in_=x_rows[:, :, first[k]:first[k] + width])
+            raws[k] = raw
+
+        def load_w(queue):
+            queue.dma_start(out=w_sb[:].bitcast(I32), in_=w_words.rearrange("g p b -> (g p) b").bitcast(I32))
+
+        def load_scales(queue, i):
+            queue.dma_start(out=w_sc[i:P:32, :].bitcast(I32), in_=sc_rows[i].bitcast(I32))
+
+        def region(banks):
+            blocks = sorted(set(2 * g + h for c, h, g in banks))
+            halves = sorted(set(c for c, h, g in banks))
+            step = blocks[1] - blocks[0] if len(blocks) > 1 else 1
+            return blocks, halves, slice(blocks[0], blocks[-1] + 1, step), slice(halves[0] * HALF, (halves[-1] + 1) * HALF)
+
+        def staging(banks, name, views):
+            blocks, halves, rows, cols = region(banks)
+            t = sb.tile([P, len(blocks), len(halves) * HALF], F32, name=name)
+            for c, h, g in banks:
+                k = halves.index(c)
+                views[(c, h, g)] = t[:, blocks.index(2 * g + h), k * HALF:(k + 1) * HALF]
+            return t, rows, cols
+
+        def load_r(k):
+            t, rows, cols = staging(r_loads[k], "r%d" % k, res)
+            nc.sync.dma_start(out=t[:], in_=r_rows[:, rows, cols])
+
+        r_loads = (((0,0,0,),),((0,0,1,),),((0,1,0,),),((0,1,1,),),((1,1,1,),),((1,1,0,),),((1,0,0,),),((1,0,1,),),)
+        stores = (((0,0,0,),),((0,0,1,),),((0,1,0,),),((0,1,1,),(1,1,1,),),((1,1,0,),),((1,0,0,),(1,0,1,),),)
+        load_w(nc.sync)
+        load_x(0)
+        load_scales(nc.sync, 0)
+        load_scales(nc.sync, 1)
+        load_x(1)
+        load_scales(nc.sync, 2)
+        load_scales(nc.sync, 3)
+        load_x(2)
+        load_x(3)
+        load_x(4)
+        for k in range(0, len(r_loads)):
+            load_r(k)
+        staged = [staging(banks, "o%d" % k, outs) for k, banks in enumerate(stores)]
 
         def round_and_group(copy, dst, src):
             copy(
@@ -75,63 +102,68 @@ def tile_rows_glin_res_kernel(tc, x, w_words, w_scales, r, out):
             )
 
         def interleave(k):
-            gt = sb.tile([P, PIECE, PACK], BF16, name="grouped%d" % k, align_bytes=64)
-            v = VEC_COLS
-            round_and_group(nc.scalar.copy, gt[:, v:, :], raws[k][:, :, v:])
+            width, v = PIECES[k]
+            gt = sb.tile([P, width, PACK], BF16, name="grouped%d" % k, align_bytes=64)
+            if v < width:
+                round_and_group(nc.scalar.copy, gt[:, v:, :], raws[k][:, :, v:])
             round_and_group(nc.vector.tensor_copy, gt[:, :v, :], raws[k][:, :, :v])
             grouped[k] = gt
 
         def quantise(k):
-            cols = slice(HALF + k * PIECE, HALF + (k + 1) * PIECE)
+            cols = slice(HALF + first[k], HALF + first[k] + PIECES[k][0])
             nc.vector.quantize_mx(
                 out=codes[:, cols].bitcast(FP8X4),
                 scales=x_sc[:, cols],
                 in_=grouped[k][:].rearrange("p n t -> p (n t)"),
             )
 
-        def multiply(c, h):
+        def multiply(c, h, g):
             window = slice(c * HALF, c * HALF + N)
-            for g in reversed([bank[2] for bank in order if bank[:2] == (c, h)]):
-                acc = ps.tile([P, N], F32, name="acc%d%d%d" % (c, h, g))
-                rows = slice(g * ROWS, (g + 1) * ROWS)
-                nc.tensor.matmul_mx(
-                    out=acc[:],
-                    lhsT=w_sb[rows, 2 * h * P:2 * (h + 1) * P].bitcast(FP4X4),
-                    lhsT_scale=w_sc[rows, h * P:(h + 1) * P],
-                    rhs=codes[rows, window].bitcast(FP8X4),
-                    rhs_scale=x_sc[rows, window],
-                    start=True,
-                    stop=True,
-                )
-                accs[(c, h, g)] = acc
+            acc = ps.tile([P, N], F32, name="acc%d%d%d" % (c, h, g))
+            rows = slice(g * ROWS, (g + 1) * ROWS)
+            nc.tensor.matmul_mx(
+                out=acc[:],
+                lhsT=w_sb[rows, 2 * h * P:2 * (h + 1) * P].bitcast(FP4X4),
+                lhsT_scale=w_sc[rows, h * P:(h + 1) * P],
+                rhs=codes[rows, window].bitcast(FP8X4),
+                rhs_scale=x_sc[rows, window],
+                start=True,
+                stop=True,
+            )
+            accs[(c, h, g)] = acc
 
-        whole = sb.tile([P, N], F32, name="whole")
-        last_pair = order[-1][:2]
-        pair = sb.tile([P, G, HALF], F32, name="pair")
+        added = set()
 
         def finish(c, h, g):
-            outputs = slice(h * P, (h + 1) * P)
-            cols = slice(c * HALF, (c + 1) * HALF)
-            sums = accs[(c, h, g)][:, HALF:]
-            if (h, g) == whole_rows:
-                nc.vector.tensor_add(out=whole[:, cols], in0=sums, in1=res[(c, h, g)])
-                if c == 1:
-                    nc.sync.dma_start(out=out[g, outputs, :], in_=whole[:])
-            elif (c, h) == last_pair:
-                nc.vector.tensor_add(out=pair[:, g, :], in0=sums, in1=res[(c, h, g)])
-                if (c, h, g) == order[-1]:
-                    nc.sync.dma_start(out=out.rearrange("g m n -> m g n")[outputs, :, cols], in_=pair[:])
-            else:
-                o = sb.tile([P, HALF], F32, name="o%d%d%d" % (c, h, g))
-                nc.vector.tensor_add(out=o[:], in0=sums, in1=res[(c, h, g)])
-                nc.sync.dma_start(out=out[g, outputs, cols], in_=o[:])
+            nc.vector.tensor_add(out=outs[(c, h, g)], in0=accs[(c, h, g)][:, HALF:], in1=res[(c, h, g)])
+            added.add((c, h, g))
+            for banks, (t, rows, cols) in zip(stores, staged):
+                if (c, h, g) in banks and all(bank in added for bank in banks):
+                    nc.sync.dma_start(out=out_rows[:, rows, cols], in_=t[:])
 
-        for c in range(2):
-            interleave(2 * c)
-            interleave(2 * c + 1)
-            quantise(2 * c)
-            quantise(2 * c + 1)
-            for h in (c, 1 - c):
-                multiply(c, h)
-        for c, h, g in order:
-            finish(c, h, g)
+        interleave(0)
+        interleave(1)
+        quantise(0)
+        quantise(1)
+        multiply(0, 0, 1)
+        multiply(0, 0, 0)
+        multiply(0, 1, 1)
+        multiply(0, 1, 0)
+        interleave(2)
+        interleave(3)
+        quantise(2)
+        interleave(4)
+        quantise(3)
+        quantise(4)
+        multiply(1, 1, 0)
+        multiply(1, 1, 1)
+        multiply(1, 0, 1)
+        multiply(1, 0, 0)
+        finish(0, 0, 0)
+        finish(0, 0, 1)
+        finish(0, 1, 0)
+        finish(0, 1, 1)
+        finish(1, 1, 1)
+        finish(1, 1, 0)
+        finish(1, 0, 0)
+        finish(1, 0, 1)

@@ -19,7 +19,7 @@ ROWS = D // PACK
 HALF = N // 2
 SCALE_ROWS = 4
 RUN = 4
-PIECES = ((128,72,),(128,72,),(128,72,),(64,40,),(64,40,),)
+PIECES = ((128,128,),(128,72,),(128,72,),(64,40,),(64,40,),)
 
 
 def tile_rows_glin_res_kernel(tc, x, w_words, w_scales, r, out):
@@ -81,11 +81,11 @@ def tile_rows_glin_res_kernel(tc, x, w_words, w_scales, r, out):
 
         r_loads = (((0,0,0,),),((0,0,1,),),((0,1,0,),),((0,1,1,),),((1,1,1,),),((1,1,0,),),((1,0,0,),),((1,0,1,),),)
         stores = (((0,0,0,),),((0,0,1,),),((0,1,0,),),((0,1,1,),(1,1,1,),),((1,1,0,),),((1,0,0,),(1,0,1,),),)
-        load_w(nc.sync)
+        load_scales(nc.scalar, 0)
         load_x(0)
-        load_scales(nc.sync, 0)
         load_scales(nc.sync, 1)
         load_x(1)
+        load_w(nc.sync)
         load_scales(nc.sync, 2)
         load_scales(nc.sync, 3)
         load_x(2)

@@ -19,7 +19,7 @@ ROWS = D // PACK
 HALF = N // 2
 SCALE_ROWS = 4
 RUN = 4
-PIECES = ((128,128,),(128,72,),(128,72,),(64,40,),(64,40,),)
+PIECES = ((128,128,),(128,72,),(192,128,),(64,40,),)
 
 
 def tile_rows_glin_res_kernel(tc, x, w_words, w_scales, r, out):
@@ -77,7 +77,11 @@ def tile_rows_glin_res_kernel(tc, x, w_words, w_scales, r, out):
 
         def load_r(k):
             t, rows, cols = staging(r_loads[k], "r%d" % k, res)
-            nc.sync.dma_start(out=t[:], in_=r_rows[:, rows, cols])
+            parts = 2 if k in (6,) else 1
+            width = HALF // parts
+            for j in range(parts):
+                first_col = cols.start + j * width
+                nc.sync.dma_start(out=t[:, :, j * width:(j + 1) * width], in_=r_rows[:, rows, first_col:first_col + width])
 
         r_loads = (((0,0,0,),),((0,0,1,),),((0,1,0,),),((0,1,1,),),((1,1,1,),),((1,1,0,),),((1,0,0,),),((1,0,1,),),)
         stores = (((0,0,0,),),((0,0,1,),),((0,1,0,),),((0,1,1,),(1,1,1,),),((1,1,0,),),((1,0,0,),(1,0,1,),),)
@@ -90,7 +94,6 @@ def tile_rows_glin_res_kernel(tc, x, w_words, w_scales, r, out):
         load_scales(nc.sync, 3)
         load_x(2)
         load_x(3)
-        load_x(4)
         for k in range(0, len(r_loads)):
             load_r(k)
         staged = [staging(banks, "o%d" % k, outs) for k, banks in enumerate(stores)]
@@ -110,12 +113,14 @@ def tile_rows_glin_res_kernel(tc, x, w_words, w_scales, r, out):
             grouped[k] = gt
 
         def quantise(k):
-            cols = slice(HALF + first[k], HALF + first[k] + PIECES[k][0])
-            nc.vector.quantize_mx(
-                out=codes[:, cols].bitcast(FP8X4),
-                scales=x_sc[:, cols],
-                in_=grouped[k][:].rearrange("p n t -> p (n t)"),
-            )
+            for lo in range(0, PIECES[k][0], 128):
+                hi = min(lo + 128, PIECES[k][0])
+                cols = slice(HALF + first[k] + lo, HALF + first[k] + hi)
+                nc.vector.quantize_mx(
+                    out=codes[:, cols].bitcast(FP8X4),
+                    scales=x_sc[:, cols],
+                    in_=grouped[k][:, lo:hi, :].rearrange("p n t -> p (n t)"),
+                )
 
         def multiply(c, h, g):
             window = slice(c * HALF, c * HALF + N)
@@ -152,9 +157,7 @@ def tile_rows_glin_res_kernel(tc, x, w_words, w_scales, r, out):
         interleave(2)
         interleave(3)
         quantise(2)
-        interleave(4)
         quantise(3)
-        quantise(4)
         multiply(1, 1, 0)
         multiply(1, 1, 1)
         multiply(1, 0, 1)

@@ -17,9 +17,16 @@ P = 128
 PACK = 4
 ROWS = D // PACK
 HALF = N // 2
+QUAD = 32
 SCALE_ROWS = 4
 RUN = 4
-PIECES = ((128,128,),(128,72,),(192,128,),(64,40,),)
+QUANT = 128
+X_LOADS = (128, 128, 192, 64)
+PARTS = (((128, 128), (128, 72)), ((192, 128), (64, 40)))
+PASSES = ((0, 0), (0, 2), (0, 1), (0, 3), (1, 3), (1, 1), (1, 0), (1, 2))
+ADDS = ((0, 0), (0, 2), (0, 1), (0, 3), (1, 3), (1, 1), (1, 0), (1, 2))
+R_LOADS = (((0,), 1), ((1,), 1), ((2,), 1), ((3,), 1), ((4,), 1), ((5,), 1), ((6,), 2), ((7,), 1))
+STORES = ((0,), (1,), (2,), (3, 4), (5,), (6, 7))
 
 
 def tile_rows_glin_res_kernel(tc, x, w_words, w_scales, r, out):
@@ -39,64 +46,49 @@ def tile_rows_glin_res_kernel(tc, x, w_words, w_scales, r, out):
         nc.vector.memset(x_sc[:, :HALF].bitcast(I32), 0)
 
         x_rows = x.rearrange("g (p j) n -> (g p) j n", j=PACK)
+        w_rows = w_words.rearrange("g p b -> (g p) b")
         sc_rows = w_scales.rearrange("g (q i) m -> i (g q) m", i=SCALE_ROWS)
         r_rows = r.rearrange("g (h p) n -> p (g h) n", p=P)
         out_rows = out.rearrange("g (h p) n -> p (g h) n", p=P)
-        first = [sum(w for w, v in PIECES[:k]) for k in range(len(PIECES))]
-        raws = {}
-        res = {}
-        accs = {}
-        grouped = {}
-        outs = {}
+        raws, grouped, accs, res, outs = {}, {}, {}, {}, {}
 
         def load_x(k):
-            width = PIECES[k][0]
-            raw = sb.tile([P, PACK, width], F32, name="raw%d" % k)
-            nc.sync.dma_start(out=raw[:], in_=x_rows[:, :, first[k]:first[k] + width])
-            raws[k] = raw
+            first = sum(X_LOADS[:k])
+            raws[k] = sb.tile([P, PACK, X_LOADS[k]], F32, name="raw%d" % k)
+            nc.sync.dma_start(out=raws[k][:], in_=x_rows[:, :, first:first + X_LOADS[k]])
 
-        def load_w(queue):
-            queue.dma_start(out=w_sb[:].bitcast(I32), in_=w_words.rearrange("g p b -> (g p) b").bitcast(I32))
+        def load_w(lo, hi):
+            nc.sync.dma_start(out=w_sb[:, 2 * lo:2 * hi].bitcast(I32), in_=w_rows[:, 2 * lo:2 * hi].bitcast(I32))
 
         def load_scales(queue, i):
-            queue.dma_start(out=w_sc[i:P:32, :].bitcast(I32), in_=sc_rows[i].bitcast(I32))
+            queue.dma_start(out=w_sc[i:P:QUAD, :].bitcast(I32), in_=sc_rows[i].bitcast(I32))
 
-        def region(banks):
-            blocks = sorted(set(2 * g + h for c, h, g in banks))
-            halves = sorted(set(c for c, h, g in banks))
-            step = blocks[1] - blocks[0] if len(blocks) > 1 else 1
-            return blocks, halves, slice(blocks[0], blocks[-1] + 1, step), slice(halves[0] * HALF, (halves[-1] + 1) * HALF)
-
-        def staging(banks, name, views):
-            blocks, halves, rows, cols = region(banks)
+        def staging(places, name, views):
+            blocks = sorted(set(ADDS[i][1] for i in places))
+            halves = sorted(set(ADDS[i][0] for i in places))
             t = sb.tile([P, len(blocks), len(halves) * HALF], F32, name=name)
-            for c, h, g in banks:
-                k = halves.index(c)
-                views[(c, h, g)] = t[:, blocks.index(2 * g + h), k * HALF:(k + 1) * HALF]
-            return t, rows, cols
+            for i in places:
+                c, b = ADDS[i]
+                j = halves.index(c)
+                views[i] = t[:, blocks.index(b), j * HALF:(j + 1) * HALF]
+            step = blocks[1] - blocks[0] if len(blocks) > 1 else 1
+            return t, slice(blocks[0], blocks[-1] + 1, step), slice(halves[0] * HALF, (halves[-1] + 1) * HALF)
 
-        def load_r(k):
-            t, rows, cols = staging(r_loads[k], "r%d" % k, res)
-            parts = 2 if k in (6,) else 1
-            width = HALF // parts
-            for j in range(parts):
-                first_col = cols.start + j * width
-                nc.sync.dma_start(out=t[:, :, j * width:(j + 1) * width], in_=r_rows[:, rows, first_col:first_col + width])
-
-        r_loads = (((0,0,0,),),((0,0,1,),),((0,1,0,),),((0,1,1,),),((1,1,1,),),((1,1,0,),),((1,0,0,),),((1,0,1,),),)
-        stores = (((0,0,0,),),((0,0,1,),),((0,1,0,),),((0,1,1,),(1,1,1,),),((1,1,0,),),((1,0,0,),(1,0,1,),),)
         load_scales(nc.scalar, 0)
         load_x(0)
         load_scales(nc.sync, 1)
         load_x(1)
-        load_w(nc.sync)
+        load_w(0, M)
         load_scales(nc.sync, 2)
         load_scales(nc.sync, 3)
         load_x(2)
         load_x(3)
-        for k in range(0, len(r_loads)):
-            load_r(k)
-        staged = [staging(banks, "o%d" % k, outs) for k, banks in enumerate(stores)]
+        for k, (places, parts) in enumerate(R_LOADS):
+            t, rows, cols = staging(places, "r%d" % k, res)
+            width = (cols.stop - cols.start) // parts
+            for lo in range(0, parts * width, width):
+                nc.sync.dma_start(out=t[:, :, lo:lo + width], in_=r_rows[:, rows, cols.start + lo:cols.start + lo + width])
+        staged = [staging(places, "o%d" % k, outs) for k, places in enumerate(STORES)]
 
         def round_and_group(copy, dst, src):
             copy(
@@ -104,30 +96,31 @@ def tile_rows_glin_res_kernel(tc, x, w_words, w_scales, r, out):
                 in_=src.rearrange("p t (c i) -> p c t i", i=RUN),
             )
 
-        def interleave(k):
-            width, v = PIECES[k]
-            gt = sb.tile([P, width, PACK], BF16, name="grouped%d" % k, align_bytes=64)
-            if v < width:
-                round_and_group(nc.scalar.copy, gt[:, v:, :], raws[k][:, :, v:])
-            round_and_group(nc.vector.tensor_copy, gt[:, :v, :], raws[k][:, :, :v])
-            grouped[k] = gt
+        def interleave(first, width, share):
+            k = max(j for j in range(len(X_LOADS)) if sum(X_LOADS[:j]) <= first)
+            lo = first - sum(X_LOADS[:k])
+            grouped[first] = sb.tile([P, width, PACK], BF16, name="grouped%d" % first, align_bytes=64)
+            if share < width:
+                round_and_group(nc.scalar.copy, grouped[first][:, share:, :], raws[k][:, :, lo + share:lo + width])
+            round_and_group(nc.vector.tensor_copy, grouped[first][:, :share, :], raws[k][:, :, lo:lo + share])
 
-        def quantise(k):
-            for lo in range(0, PIECES[k][0], 128):
-                hi = min(lo + 128, PIECES[k][0])
-                cols = slice(HALF + first[k] + lo, HALF + first[k] + hi)
+        def quantise(first, width):
+            for lo in range(0, width, QUANT):
+                hi = min(lo + QUANT, width)
+                cols = slice(HALF + first + lo, HALF + first + hi)
                 nc.vector.quantize_mx(
                     out=codes[:, cols].bitcast(FP8X4),
                     scales=x_sc[:, cols],
-                    in_=grouped[k][:, lo:hi, :].rearrange("p n t -> p (n t)"),
+                    in_=grouped[first][:, lo:hi, :].rearrange("p n t -> p (n t)"),
                 )
 
-        def multiply(c, h, g):
+        def multiply(c, b):
+            g, h = divmod(b, 2)
             window = slice(c * HALF, c * HALF + N)
-            acc = ps.tile([P, N], F32, name="acc%d%d%d" % (c, h, g))
             rows = slice(g * ROWS, (g + 1) * ROWS)
+            accs[(c, b)] = ps.tile([P, N], F32, name="acc%d%d" % (c, b))
             nc.tensor.matmul_mx(
-                out=acc[:],
+                out=accs[(c, b)][:],
                 lhsT=w_sb[rows, 2 * h * P:2 * (h + 1) * P].bitcast(FP4X4),
                 lhsT_scale=w_sc[rows, h * P:(h + 1) * P],
                 rhs=codes[rows, window].bitcast(FP8X4),
@@ -135,38 +128,19 @@ def tile_rows_glin_res_kernel(tc, x, w_words, w_scales, r, out):
                 start=True,
                 stop=True,
             )
-            accs[(c, h, g)] = acc
 
-        added = set()
+        for c, parts in enumerate(PARTS):
+            firsts = [c * HALF + sum(width for width, share in parts[:j]) for j in range(len(parts))]
+            for first, (width, share) in zip(firsts, parts):
+                interleave(first, width, share)
+            for first, (width, share) in zip(firsts, parts):
+                quantise(first, width)
+            for half, b in PASSES:
+                if half == c:
+                    multiply(c, b)
 
-        def finish(c, h, g):
-            nc.vector.tensor_add(out=outs[(c, h, g)], in0=accs[(c, h, g)][:, HALF:], in1=res[(c, h, g)])
-            added.add((c, h, g))
-            for banks, (t, rows, cols) in zip(stores, staged):
-                if (c, h, g) in banks and all(bank in added for bank in banks):
+        for i, (c, b) in enumerate(ADDS):
+            nc.vector.tensor_add(out=outs[i], in0=accs[(c, b)][:, HALF:], in1=res[i])
+            for places, (t, rows, cols) in zip(STORES, staged):
+                if i == max(places):
                     nc.sync.dma_start(out=out_rows[:, rows, cols], in_=t[:])
-
-        interleave(0)
-        interleave(1)
-        quantise(0)
-        quantise(1)
-        multiply(0, 0, 1)
-        multiply(0, 0, 0)
-        multiply(0, 1, 1)
-        multiply(0, 1, 0)
-        interleave(2)
-        interleave(3)
-        quantise(2)
-        quantise(3)
-        multiply(1, 1, 0)
-        multiply(1, 1, 1)
-        multiply(1, 0, 1)
-        multiply(1, 0, 0)
-        finish(0, 0, 0)
-        finish(0, 0, 1)
-        finish(0, 1, 0)
-        finish(0, 1, 1)
-        finish(1, 1, 1)
-        finish(1, 1, 0)
-        finish(1, 0, 0)
-        finish(1, 0, 1)

@@ -23,8 +23,7 @@ RUN = 4
 QUANT = 128
 X_LOADS = (128, 128, 192, 64)
 PARTS = (((128, 128), (128, 72)), ((192, 128), (64, 40)))
-PASSES = ((0, 0), (0, 2), (0, 1), (0, 3), (1, 3), (1, 1), (1, 0), (1, 2))
-ADDS = ((0, 0), (0, 2), (0, 1), (0, 3), (1, 3), (1, 1), (1, 0), (1, 2))
+BANKS = ((0, 0), (0, 2), (0, 1), (0, 3), (1, 3), (1, 1), (1, 0), (1, 2))
 R_LOADS = (((0,), 1), ((1,), 1), ((2,), 1), ((3,), 1), ((4,), 1), ((5,), 1), ((6,), 2), ((7,), 1))
 STORES = ((0,), (1,), (2,), (3, 4), (5,), (6, 7))
 
@@ -52,42 +51,45 @@ def tile_rows_glin_res_kernel(tc, x, w_words, w_scales, r, out):
         out_rows = out.rearrange("g (h p) n -> p (g h) n", p=P)
         raws, grouped, accs, res, outs = {}, {}, {}, {}, {}
 
-        def load_x(k):
+        def load_x(queue, k):
             first = sum(X_LOADS[:k])
             raws[k] = sb.tile([P, PACK, X_LOADS[k]], F32, name="raw%d" % k)
-            nc.sync.dma_start(out=raws[k][:], in_=x_rows[:, :, first:first + X_LOADS[k]])
+            queue.dma_start(out=raws[k][:], in_=x_rows[:, :, first:first + X_LOADS[k]])
 
-        def load_w(lo, hi):
-            nc.sync.dma_start(out=w_sb[:, 2 * lo:2 * hi].bitcast(I32), in_=w_rows[:, 2 * lo:2 * hi].bitcast(I32))
+        def load_w(queue):
+            queue.dma_start(out=w_sb[:].bitcast(I32), in_=w_rows.bitcast(I32))
 
         def load_scales(queue, i):
             queue.dma_start(out=w_sc[i:P:QUAD, :].bitcast(I32), in_=sc_rows[i].bitcast(I32))
 
         def staging(places, name, views):
-            blocks = sorted(set(ADDS[i][1] for i in places))
-            halves = sorted(set(ADDS[i][0] for i in places))
+            blocks = sorted(set(BANKS[i][1] for i in places))
+            halves = sorted(set(BANKS[i][0] for i in places))
             t = sb.tile([P, len(blocks), len(halves) * HALF], F32, name=name)
             for i in places:
-                c, b = ADDS[i]
+                c, b = BANKS[i]
                 j = halves.index(c)
                 views[i] = t[:, blocks.index(b), j * HALF:(j + 1) * HALF]
             step = blocks[1] - blocks[0] if len(blocks) > 1 else 1
             return t, slice(blocks[0], blocks[-1] + 1, step), slice(halves[0] * HALF, (halves[-1] + 1) * HALF)
 
-        load_scales(nc.scalar, 0)
-        load_x(0)
-        load_scales(nc.sync, 1)
-        load_x(1)
-        load_w(0, M)
-        load_scales(nc.sync, 2)
-        load_scales(nc.sync, 3)
-        load_x(2)
-        load_x(3)
-        for k, (places, parts) in enumerate(R_LOADS):
+        def load_r(queue, k):
+            places, parts = R_LOADS[k]
             t, rows, cols = staging(places, "r%d" % k, res)
             width = (cols.stop - cols.start) // parts
             for lo in range(0, parts * width, width):
-                nc.sync.dma_start(out=t[:, :, lo:lo + width], in_=r_rows[:, rows, cols.start + lo:cols.start + lo + width])
+                queue.dma_start(out=t[:, :, lo:lo + width], in_=r_rows[:, rows, cols.start + lo:cols.start + lo + width])
+
+        load_x(nc.sync, 0)
+        load_scales(nc.sync, 0)
+        load_x(nc.sync, 1)
+        load_w(nc.sync)
+        for i in range(1, SCALE_ROWS):
+            load_scales(nc.sync, i)
+        load_x(nc.sync, 2)
+        load_x(nc.sync, 3)
+        for k in range(len(R_LOADS)):
+            load_r(nc.sync, k)
         staged = [staging(places, "o%d" % k, outs) for k, places in enumerate(STORES)]
 
         def round_and_group(copy, dst, src):
@@ -102,7 +104,8 @@ def tile_rows_glin_res_kernel(tc, x, w_words, w_scales, r, out):
             grouped[first] = sb.tile([P, width, PACK], BF16, name="grouped%d" % first, align_bytes=64)
             if share < width:
                 round_and_group(nc.scalar.copy, grouped[first][:, share:, :], raws[k][:, :, lo + share:lo + width])
-            round_and_group(nc.vector.tensor_copy, grouped[first][:, :share, :], raws[k][:, :, lo:lo + share])
+            if share > 0:
+                round_and_group(nc.vector.tensor_copy, grouped[first][:, :share, :], raws[k][:, :, lo:lo + share])
 
         def quantise(first, width):
             for lo in range(0, width, QUANT):
@@ -135,11 +138,11 @@ def tile_rows_glin_res_kernel(tc, x, w_words, w_scales, r, out):
                 interleave(first, width, share)
             for first, (width, share) in zip(firsts, parts):
                 quantise(first, width)
-            for half, b in PASSES:
+            for half, b in BANKS:
                 if half == c:
                     multiply(c, b)
 
-        for i, (c, b) in enumerate(ADDS):
+        for i, (c, b) in enumerate(BANKS):
             nc.vector.tensor_add(out=outs[i], in0=accs[(c, b)][:, HALF:], in1=res[i])
             for places, (t, rows, cols) in zip(STORES, staged):
                 if i == max(places):

from contextlib import ExitStack

import concourse.mybir as mybir

G, D, M, N = 2, 256, 256, 512
FLOPS = 2 * G * D * M * N

F32 = mybir.dt.float32
BF16 = mybir.dt.bfloat16
I32 = mybir.dt.int32
U32 = mybir.dt.uint32
U8 = mybir.dt.uint8
FP8X4 = mybir.dt.float8_e4m3fn_x4
FP4X4 = mybir.dt.float4_e2m1fn_x4

P = 128
PACK = 4
ROWS = D // PACK
HALF = N // 2
QUAD = 32
SCALE_ROWS = 4
RUN = 4
QUANT = 128
X_LOADS = (128, 128, 192, 64)
PARTS = (((128, 128), (128, 72)), ((192, 128), (64, 40)))
BANKS = ((0, 0), (0, 2), (0, 1), (0, 3), (1, 3), (1, 1), (1, 0), (1, 2))
R_LOADS = (((0,), 1), ((1,), 1), ((2,), 1), ((3,), 1), ((4,), 1), ((5,), 1), ((6,), 2), ((7,), 1))
STORES = ((0,), (1,), (2,), (3, 4), (5,), (6, 7))


def tile_rows_glin_res_kernel(tc, x, w_words, w_scales, r, out):
    nc = tc.nc
    with ExitStack() as ctx:
        sb = ctx.enter_context(tc.tile_pool(name="sb", bufs=1))
        ps = ctx.enter_context(tc.psum_pool(name="ps", bufs=1))
        ctx.enter_context(tc.manual_schedule())

        w_sb = sb.tile([P, 2 * M], U8, name="w_sb", align_bytes=64)
        w_sc = sb.tile([P, M], U8, name="w_sc", align_bytes=64)
        codes = sb.tile([P, HALF + N], U32, name="codes", align_bytes=64)
        x_sc = sb.tile([P, HALF + N], U8, name="x_sc", align_bytes=64)

        nc.vector.memset(w_sc[:].bitcast(I32), 0)
        nc.vector.memset(codes[:, :HALF], 0)
        nc.vector.memset(x_sc[:, :HALF].bitcast(I32), 0)

        x_rows = x.rearrange("g (p j) n -> (g p) j n", j=PACK)
        w_rows = w_words.rearrange("g p b -> (g p) b")
        sc_rows = w_scales.rearrange("g (q i) m -> i (g q) m", i=SCALE_ROWS)
        r_rows = r.rearrange("g (h p) n -> p (g h) n", p=P)
        out_rows = out.rearrange("g (h p) n -> p (g h) n", p=P)
        raws, grouped, accs, res, outs = {}, {}, {}, {}, {}

        def load_x(queue, k):
            first = sum(X_LOADS[:k])
            raws[k] = sb.tile([P, PACK, X_LOADS[k]], F32, name="raw%d" % k)
            queue.dma_start(out=raws[k][:], in_=x_rows[:, :, first:first + X_LOADS[k]])

        def load_w(queue):
            queue.dma_start(out=w_sb[:].bitcast(I32), in_=w_rows.bitcast(I32))

        def load_scales(queue, i):
            queue.dma_start(out=w_sc[i:P:QUAD, :].bitcast(I32), in_=sc_rows[i].bitcast(I32))

        def staging(places, name, views):
            blocks = sorted(set(BANKS[i][1] for i in places))
            halves = sorted(set(BANKS[i][0] for i in places))
            t = sb.tile([P, len(blocks), len(halves) * HALF], F32, name=name)
            for i in places:
                c, b = BANKS[i]
                j = halves.index(c)
                views[i] = t[:, blocks.index(b), j * HALF:(j + 1) * HALF]
            step = blocks[1] - blocks[0] if len(blocks) > 1 else 1
            return t, slice(blocks[0], blocks[-1] + 1, step), slice(halves[0] * HALF, (halves[-1] + 1) * HALF)

        def load_r(queue, k):
            places, parts = R_LOADS[k]
            t, rows, cols = staging(places, "r%d" % k, res)
            width = (cols.stop - cols.start) // parts
            for lo in range(0, parts * width, width):
                queue.dma_start(out=t[:, :, lo:lo + width], in_=r_rows[:, rows, cols.start + lo:cols.start + lo + width])

        load_x(nc.sync, 0)
        load_scales(nc.sync, 0)
        load_x(nc.sync, 1)
        load_w(nc.sync)
        for i in range(1, SCALE_ROWS):
            load_scales(nc.sync, i)
        load_x(nc.sync, 2)
        load_x(nc.sync, 3)
        for k in range(len(R_LOADS)):
            load_r(nc.sync, k)
        staged = [staging(places, "o%d" % k, outs) for k, places in enumerate(STORES)]

        def round_and_group(copy, dst, src):
            copy(
                out=dst.rearrange("p (c i) t -> p c t i", i=RUN),
                in_=src.rearrange("p t (c i) -> p c t i", i=RUN),
            )

        def interleave(first, width, share):
            k = max(j for j in range(len(X_LOADS)) if sum(X_LOADS[:j]) <= first)
            lo = first - sum(X_LOADS[:k])
            grouped[first] = sb.tile([P, width, PACK], BF16, name="grouped%d" % first, align_bytes=64)
            if share < width:
                round_and_group(nc.scalar.copy, grouped[first][:, share:, :], raws[k][:, :, lo + share:lo + width])
            if share > 0:
                round_and_group(nc.vector.tensor_copy, grouped[first][:, :share, :], raws[k][:, :, lo:lo + share])

        def quantise(first, width):
            for lo in range(0, width, QUANT):
                hi = min(lo + QUANT, width)
                cols = slice(HALF + first + lo, HALF + first + hi)
                nc.vector.quantize_mx(
                    out=codes[:, cols].bitcast(FP8X4),
                    scales=x_sc[:, cols],
                    in_=grouped[first][:, lo:hi, :].rearrange("p n t -> p (n t)"),
                )

        def multiply(c, b):
            g, h = divmod(b, 2)
            window = slice(c * HALF, c * HALF + N)
            rows = slice(g * ROWS, (g + 1) * ROWS)
            accs[(c, b)] = ps.tile([P, N], F32, name="acc%d%d" % (c, b))
            nc.tensor.matmul_mx(
                out=accs[(c, b)][:],
                lhsT=w_sb[rows, 2 * h * P:2 * (h + 1) * P].bitcast(FP4X4),
                lhsT_scale=w_sc[rows, h * P:(h + 1) * P],
                rhs=codes[rows, window].bitcast(FP8X4),
                rhs_scale=x_sc[rows, window],
                start=True,
                stop=True,
            )

        for c, parts in enumerate(PARTS):
            firsts = [c * HALF + sum(width for width, share in parts[:j]) for j in range(len(parts))]
            for first, (width, share) in zip(firsts, parts):
                interleave(first, width, share)
            for first, (width, share) in zip(firsts, parts):
                quantise(first, width)
            for half, b in BANKS:
                if half == c:
                    multiply(c, b)

        for i, (c, b) in enumerate(BANKS):
            nc.vector.tensor_add(out=outs[i], in0=accs[(c, b)][:, HALF:], in1=res[i])
            for places, (t, rows, cols) in zip(STORES, staged):
                if i == max(places):
                    nc.sync.dma_start(out=out_rows[:, rows, cols], in_=t[:])
